import numpy as np
import ml_dtypes


def mxq(x, axis, fmt="e4m3"):
    dtype, down = {"e4m3": (ml_dtypes.float8_e4m3fn, 7), "e5m2": (ml_dtypes.float8_e5m2, 14)}[fmt]
    v = np.moveaxis(np.asarray(x, np.float32).astype(ml_dtypes.bfloat16).astype(np.float64), axis, -1)
    blocks = v.reshape(v.shape[:-1] + (-1, 32))
    amax = np.abs(blocks).max(-1, keepdims=True)
    byte = np.maximum(np.where(amax > 0, np.frexp(amax)[1] - 1 + 127, 0) - down, 1)
    scale = np.exp2(byte - 127.0)
    codes = (blocks / scale).astype(np.float32).astype(dtype).astype(np.float64)
    return np.moveaxis((codes * scale).reshape(v.shape), -1, axis)


WIDE = False


def mx_kscale(k):
    if not WIDE:
        return np.ones(k)
    levels = np.array([10, -10, 5, -5, 0])
    if k % 512:
        return np.exp2(np.random.permutation(np.resize(levels, k // 32))).repeat(32)
    a = np.empty((k // 512, 16))
    for p in range(k // 512):
        a[p, :8] = np.random.permutation(np.resize(levels, 8))
        for g in range(8):
            far = levels[np.abs(levels - a[p, g]) >= 10]
            a[p, g + 8] = far[np.random.randint(len(far))]
    return np.exp2(a.ravel()).repeat(32)


def f64(x):
    return np.asarray(x).astype(np.float64)


def striped(idx):
    return np.tile(idx.reshape(-1, 16).T, (8, 1)).astype(np.uint16)


def unstriped(offs):
    return offs[:16].T.reshape(-1).astype(np.int64)


def striped8(idx):
    return np.concatenate([x.reshape(-1, 16).T for x in idx]).astype(np.uint16)


def runs(offs, k):
    lists = np.stack([offs[16 * r : 16 * r + 16].T.reshape(-1) for r in range(8)]).astype(np.int64)
    return lists[np.arange(k) % 512 // 64]


def pack_weight(w):
    k, n = w.shape
    w = f64(np.asarray(w, np.float32).astype(ml_dtypes.bfloat16)).reshape(k // 32, 32, n)
    amax = np.abs(w).max(1)
    byte = np.clip(np.where(amax > 0, np.frexp(amax)[1] - 1 + 127 - 7, 1), 1, 254)
    scaled = (w * np.exp2(127.0 - byte)[:, None, :]).reshape(k, n).astype(np.float32)
    words = np.ascontiguousarray(scaled.reshape(k // 512, 128, 4, n).transpose(0, 1, 3, 2)).astype(ml_dtypes.float8_e4m3fn).view(np.uint8)
    return words, np.ascontiguousarray(byte.astype(np.uint8).reshape(k // 512, 16, n))


def unpack_weight(words, scales):
    g, p, n, _ = words.shape
    vals = np.ascontiguousarray(words).view(ml_dtypes.float8_e4m3fn).astype(np.float64) * np.repeat(np.exp2(scales.astype(np.float64) - 127.0), 8, axis=1)[..., None]
    return vals.transpose(0, 1, 3, 2).reshape(g * 512, n)


E2M1 = np.array([0.0, 0.5, 1.0, 1.5, 2.0, 3.0, 4.0, 6.0, -0.0, -0.5, -1.0, -1.5, -2.0, -3.0, -4.0, -6.0])


def pack_fp4(w):
    k, n = w.shape
    w = f64(np.asarray(w, np.float32).astype(ml_dtypes.bfloat16)).reshape(k // 32, 32, n)
    amax = np.abs(w).max(1)
    mant, ex = np.frexp(amax / 6.0)
    byte = np.clip(np.where(amax > 0, np.where(mant > 0.5, ex, ex - 1) + 127, 1), 1, 254)
    scaled = (w * np.exp2(127.0 - byte)[:, None, :]).reshape(k, n).astype(np.float32)
    c = np.ascontiguousarray(scaled.reshape(k // 512, 128, 4, n).transpose(0, 1, 3, 2)).astype(ml_dtypes.float4_e2m1fn).view(np.uint8) & 0xF
    words = (c[..., 0::2] | (c[..., 1::2] << 4)).reshape(k // 512, 128, 2 * n)
    return np.ascontiguousarray(words), np.ascontiguousarray(byte.astype(np.uint8).reshape(k // 512, 16, n))


def unpack_fp4(words, scales):
    g, _, n = scales.shape
    words = np.ascontiguousarray(words).reshape(g, 128, n, 2)
    nib = np.empty((g, 128, n, 4), np.uint8)
    nib[..., 0::2] = words & 0xF
    nib[..., 1::2] = words >> 4
    vals = E2M1[nib] * np.repeat(np.exp2(scales.astype(np.float64) - 127.0), 8, axis=1)[..., None]
    return vals.transpose(0, 1, 3, 2).reshape(g * 512, n)


def sigmoid(v):
    return 1.0 / (1.0 + np.exp(-np.maximum(v, -700.0)))

def planes(y):
    n, m = y.shape
    v = y.astype(np.float32).astype(ml_dtypes.bfloat16).astype(np.float64).reshape(n // 32, 32, m)
    top = np.abs(v).max(1)
    byte = np.clip(np.where(top > 0, np.frexp(top)[1] - 1 + 127 - 7, 1), 1, 254)
    codes = (v * np.exp2(127.0 - byte)[:, None, :]).reshape(n, m).astype(np.float32).astype(ml_dtypes.float8_e4m3fn).view(np.uint8)
    words = codes.reshape(n // 512, 128, 4, m).transpose(0, 1, 3, 2)
    return np.ascontiguousarray(words), np.ascontiguousarray(byte.astype(np.uint8).reshape(n // 512, 16, m))


K, T, S, N, H, C, W = 512, 2048, 512, 512, 512, 512, 256


def setup_inputs():
    n = np.random.standard_normal
    s = mx_kscale(K)[:, None]
    u = mx_kscale(S)
    packed_xT = pack_weight(n((K, T)) * s)
    packed_w1 = pack_fp4(n((K, H)) / np.sqrt(K) / s)
    packed_w2 = pack_fp4(n((K, H)) / np.sqrt(K) / s)
    packed_w3 = pack_fp4(n((H, N)) / np.sqrt(H) / u[:, None])
    return {
        "x_words": packed_xT[0],
        "x_scales": packed_xT[1],
        "w1_words": packed_w1[0],
        "w1_scales": packed_w1[1],
        "w2_words": packed_w2[0],
        "w2_scales": packed_w2[1],
        "gn": (np.random.uniform(0.5, 1.5, (H, 1)) * u[:, None]).astype(np.float32),
        "w3_words": packed_w3[0],
        "w3_scales": packed_w3[1],
        "gs": (np.random.uniform(0.5, 1.5, (K, 1)) / s).astype(np.float32),
        "offs": striped(np.random.permutation(T)[:S]),
        "two": striped(np.random.permutation(T)[:S]),
        "n1": striped(np.random.permutation(S)),
        "n2": striped(np.random.permutation(S)),
        "n3": striped8(np.stack([np.random.permutation(S) for _ in range(8)])),
        "n4": striped8(np.stack([np.random.permutation(S) for _ in range(8)])),
        "n5": striped8(np.stack([np.random.permutation(S) for _ in range(8)])),
        "cand": striped(np.random.permutation(T)[:C]),
        "n6": striped8(np.stack([np.random.permutation(S)[:W] for _ in range(8)])),
        "n7": striped8(np.stack([np.random.permutation(S)[:W] for _ in range(8)])),
    }


def reference(x_words, x_scales, w1_words, w1_scales, w2_words, w2_scales, gn, w3_words, w3_scales, gs, offs, two, n1, n2, n3, n4, n5, cand, n6, n7):
    x_cand = unpack_weight(x_words, x_scales)[:, unstriped(cand)]
    x_two = unpack_weight(x_words, x_scales)[:, unstriped(two)]
    d = unpack_fp4(w2_words, w2_scales).T @ x_two
    pa = d[np.arange(H)[:, None], runs(n3, H)]
    z2 = f64(gs) * (pa + (sigmoid(d[np.arange(H)[:, None], runs(n4, H)])) * (d[np.arange(H)[:, None], runs(n5, H)] - pa))
    b = 0.0625 * ((x_cand.T @ mxq(z2, 0, "e4m3")))
    xq = unpack_weight(x_words, x_scales)[:, unstriped(offs)]
    y = unpack_fp4(w1_words, w1_scales).T @ xq
    z = f64(gn) * (np.maximum(y * (sigmoid(y[:, unstriped(n1)])), y[:, unstriped(n2)]))
    a = unpack_fp4(w3_words, w3_scales).T @ mxq(z, 0, "e4m3")
    ra = b[np.arange(C)[:, None], runs(n7, C)] - (0.5 * (a[np.arange(N)[:, None], runs(n6, N)]))
    out = a.copy()
    out[np.arange(C)[:, None], runs(n6, C)] = ra
    return (out,) + planes(out)

@@ -1,0 +1,244 @@
+from contextlib import ExitStack
+
+import concourse.mybir as mybir
+
+F32 = mybir.dt.float32
+BF16 = mybir.dt.bfloat16
+I32 = mybir.dt.int32
+U32 = mybir.dt.uint32
+U16 = mybir.dt.uint16
+U8 = mybir.dt.uint8
+FP8X4 = mybir.dt.float8_e4m3fn_x4
+FP4X4 = mybir.dt.float4_e2m1fn_x4
+ALU = mybir.AluOpType
+ACT = mybir.ActivationFunctionType
+
+P = 128
+PACK = 4
+T = 2048
+S = 512
+W = 256
+HALF = S // 2
+FLOPS = 4 * 2 * 512 * 512 * 512
+
+
+def tile_picked_tfcdputbgmaxlerp_none_po_kernel(
+    tc, x_words, x_scales, w1_words, w1_scales, w2_words, w2_scales, gn, w3_words, w3_scales, gs,
+    offs, two, n1, n2, n3, n4, n5, cand, n6, n7, out_0, out_1, out_2,
+):
+    nc = tc.nc
+    with ExitStack() as ctx:
+        sb = ctx.enter_context(tc.tile_pool(name="sb", bufs=1))
+        ps = ctx.enter_context(tc.psum_pool(name="ps", bufs=1))
+
+        def tile(name, shape, dtype):
+            return sb.tile(shape, dtype, name=name, align_bytes=64)
+
+        def load_list(name, src):
+            t = sb.tile(list(src.shape), U16, name=name)
+            nc.sync.dma_start(t[:], src)
+            return t
+
+        def load_scale_rows(dst, src):
+            for q in range(4):
+                nc.sync.dma_start(dst[32 * q : 32 * q + 4, :].bitcast(I32), src[0, 4 * q : 4 * q + 4, :].bitcast(I32))
+
+        def load_weight_words(name, src):
+            raw = tile(name, [P, 2 * S], U8)
+            nc.sync.dma_start(raw[:].bitcast(I32), src[0].bitcast(I32))
+            return raw
+
+        def deal_words(name, raw):
+            dealt = tile(name, [P, 2 * S], U8)
+            nc.scalar.copy(
+                out=dealt[:].bitcast(U16).rearrange("p (t m) -> p t m", t=PACK),
+                in_=raw[:].bitcast(U16).rearrange("p (m t) -> p t m", t=PACK),
+            )
+            return dealt
+
+        def deal_scales(name, raw):
+            dealt = tile(name, [P, S], U8)
+            nc.vector.tensor_copy(
+                out=dealt[:].rearrange("p (t m) -> p t m", t=PACK),
+                in_=raw[:].rearrange("p (m t) -> p t m", t=PACK),
+            )
+            return dealt
+
+        def half(lst, h):
+            return lst[:, 16 * h : 16 * (h + 1)]
+
+        def cols(h):
+            return slice(HALF * h, HALF * (h + 1))
+
+        def woven(ap):
+            return ap.rearrange("p (c i t) -> p c t i", i=4, t=PACK)
+
+        def by_fours(ap):
+            return ap.rearrange("p t (c i) -> p c t i", i=4)
+
+        xw = tile("xw", [P, T], U32)
+        xs = tile("xs", [P, T], U8)
+        wsr = [sb.tile([P, S], U8, name=f"wsr{i}", tag=f"shared{i}", align_bytes=64) for i in range(3)]
+        nc.gpsimd.memset(xs[:].bitcast(I32), 0)
+        for i in range(3):
+            nc.vector.memset(wsr[i][:].bitcast(I32), 0)
+        l_offs = load_list("l_offs", offs)
+        l_two = load_list("l_two", two)
+        load_scale_rows(xs, x_scales)
+        nc.sync.dma_start(xw[:].bitcast(I32), x_words[0].rearrange("p c r -> p (c r)").bitcast(I32))
+        w1r = load_weight_words("w1r", w1_words)
+        w2r = load_weight_words("w2r", w2_words)
+        w3r = load_weight_words("w3r", w3_words)
+        load_scale_rows(wsr[0], w1_scales)
+        l_cand = load_list("l_cand", cand)
+        l_n1 = load_list("l_n1", n1)
+        l_n2 = load_list("l_n2", n2)
+        load_scale_rows(wsr[1], w2_scales)
+        gn_t = tile("gn_t", [P, PACK], F32)
+        gs_t = tile("gs_t", [P, PACK], F32)
+        nc.sync.dma_start(gs_t[:], gs.rearrange("(p t) o -> p (t o)", t=PACK))
+        nc.sync.dma_start(gn_t[:], gn.rearrange("(p t) o -> p (t o)", t=PACK))
+        load_scale_rows(wsr[2], w3_scales)
+        l_n3 = load_list("l_n3", n3)
+        l_n5 = load_list("l_n5", n5)
+        l_n4 = load_list("l_n4", n4)
+        l_n6 = load_list("l_n6", n6)
+        l_n7 = load_list("l_n7", n7)
+
+        bank_ya = [ps.tile([P, S], F32, name=f"bank_ya{t}") for t in range(PACK)]
+        bank_db = [ps.tile([P, S], F32, name=f"bank_db{t}") for t in range(PACK)]
+
+        def pick(name, lst, dealt, tag):
+            words = sb.tile([P, S], U32, name=name + "_w", tag=tag, align_bytes=64)
+            scales = tile(name + "_s", [P, S], U8)
+            ow, os_ = words[:], scales[:]
+            if dealt:
+                ow = ow.rearrange("p (t m) -> p m t", t=PACK)
+                os_ = os_.rearrange("p (t m) -> p m t", t=PACK)
+            nc.vector.tensor_copy(os_, xs[:].indirect(lst[:]))
+            nc.vector.tensor_copy(ow, xw[:].indirect(lst[:]))
+            return words, scales
+
+        def layer(banks, w_words, w_scales, words, scales, c):
+            for t in range(PACK):
+                nc.tensor.matmul_mx(
+                    out=banks[t][:, c],
+                    lhsT=w_words[:, 2 * P * t : 2 * P * (t + 1)].bitcast(FP4X4),
+                    lhsT_scale=w_scales[:, P * t : P * (t + 1)],
+                    rhs=words[:, c].bitcast(FP8X4),
+                    rhs_scale=scales[:, c],
+                    start=True,
+                    stop=True,
+                )
+
+        whole = slice(0, S)
+        w1w = deal_words("w1w", w1r)
+        w2w = deal_words("w2w", w2r)
+        w3w = deal_words("w3w", w3r)
+        w1s = deal_scales("w1s", wsr[0])
+        xo_w, xo_s = pick("xo", l_offs, False, "xo_w")
+        layer(bank_ya, w1w, w1s, xo_w, xo_s, whole)
+        w2s = deal_scales("w2s", wsr[1])
+        xt_w, xt_s = pick("xt", l_two, False, "shared0")
+        layer(bank_db, w2w, w2s, xt_w, xt_s, whole)
+        xc_w, xc_s = pick("xc", l_cand, True, "xc_w")
+
+        y = [tile(f"y{t}", [P, S], F32) for t in range(PACK)]
+        sig_y0 = tile("sig_y0", [P, S], F32)
+        nc.scalar.activation(out=sig_y0[:], in_=bank_ya[0][:], func=ACT.Sigmoid)
+        for t in range(PACK):
+            nc.scalar.copy(out=y[t][:], in_=bank_ya[t][:])
+
+        gs_inv = tile("gs_inv", [P, PACK], F32)
+        gs_safe = tile("gs_safe", [P, PACK], F32)
+        nc.vector.scalar_tensor_tensor(gs_safe[:], gs_t[:], 0.0, gs_t[:], ALU.is_equal, ALU.add)
+        nc.vector.reciprocal(gs_inv[:], gs_safe[:])
+
+        z_w = tile("z_w", [P, S], U32)
+        z_s = tile("z_s", [P, S], U8)
+        w3s = deal_scales("w3s", wsr[2])
+        gn_b = gn_t[:].rearrange("p (c t i) -> p c t i", c=1, i=1).to_broadcast([P, HALF // 4, PACK, 4])
+        dg = [tile(f"dg{t}", [P, S], F32) for t in range(PACK)]
+        for h in range(2):
+            gated = tile(f"gated{h}", [P, PACK, HALF], F32)
+            other = tile(f"other{h}", [P, PACK, HALF], F32)
+            nc.vector.tensor_tensor(gated[:, 0, :], sig_y0[:].indirect(half(l_n1, h)), y[0][:, cols(h)], ALU.mult)
+            for t in range(1, PACK):
+                nc.scalar.activation(out=gated[:, t, :], in_=y[t][:].indirect(half(l_n1, h)), func=ACT.Sigmoid)
+                nc.vector.tensor_tensor(gated[:, t, :], gated[:, t, :], y[t][:, cols(h)], ALU.mult)
+            for t in range(PACK - 1):
+                nc.scalar.activation(out=other[:, t, :], in_=y[t][:].indirect(half(l_n2, h)), func=ACT.Copy)
+            nc.vector.tensor_copy(other[:, PACK - 1, :], y[PACK - 1][:].indirect(half(l_n2, h)))
+            nc.vector.tensor_tensor(gated[:], gated[:], other[:], ALU.max)
+            z_bf = tile(f"z_bf{h}", [P, PACK * HALF], BF16)
+            nc.vector.tensor_tensor(woven(z_bf[:]), by_fours(gated[:]), gn_b, ALU.mult)
+            nc.vector.quantize_mx(out=z_w[:, cols(h)].bitcast(FP8X4), scales=z_s[:, cols(h)], in_=z_bf[:])
+            layer(bank_ya, w3w, w3s, z_w, z_s, cols(h))
+
+        nc.vector.tensor_scalar(dg[0][:], bank_db[0][:], gs_t[:, 0:1], None, ALU.mult)
+        for t in range(1, PACK):
+            nc.scalar.activation(out=dg[t][:], in_=bank_db[t][:], func=ACT.Copy, scale=gs_t[:, t : t + 1])
+        b = [tile(f"b{t}", [P, S], F32) for t in range(PACK)]
+        res = [tile(f"res{t}", [P, S], F32) for t in range(PACK)]
+        z2_w = tile("z2_w", [P, S], U32)
+        z2_s = tile("z2_s", [P, S], U8)
+        for h in range(2):
+            pa = tile(f"pa{h}", [P, PACK, HALF], F32)
+            mix = tile(f"mix{h}", [P, PACK, HALF], F32)
+            diff = tile(f"diff{h}", [P, PACK, HALF], F32)
+            for t in range(PACK):
+                nc.scalar.activation(out=pa[:, t, :], in_=dg[t][:].indirect(half(l_n3, h)), func=ACT.Copy)
+                nc.vector.tensor_tensor(diff[:, t, :], dg[t][:].indirect(half(l_n5, h)), pa[:, t, :], ALU.subtract)
+            for t in range(PACK):
+                nc.scalar.activation(
+                    out=mix[:, t, :], in_=dg[t][:].indirect(half(l_n4, h)), func=ACT.Sigmoid, scale=gs_inv[:, t : t + 1]
+                )
+            if h == 1:
+                for t in range(PACK):
+                    nc.scalar.activation(out=b[t][:, cols(0)], in_=bank_db[t][:, cols(0)], func=ACT.Copy, scale=0.0625)
+            for ts in (slice(0, PACK - 1), slice(PACK - 1, PACK)):
+                nc.vector.tensor_tensor(diff[:, ts, :], diff[:, ts, :], mix[:, ts, :], ALU.mult)
+            z2_bf = tile(f"z2_bf{h}", [P, PACK * HALF], BF16)
+            nc.vector.tensor_tensor(woven(z2_bf[:]), by_fours(diff[:]), by_fours(pa[:]), ALU.add)
+            nc.vector.quantize_mx(out=z2_w[:, cols(h)].bitcast(FP8X4), scales=z2_s[:, cols(h)], in_=z2_bf[:])
+            for t in range(PACK):
+                nc.tensor.matmul_mx(
+                    out=bank_db[t][:, cols(h)],
+                    lhsT=xc_w[:, P * t : P * (t + 1)].bitcast(FP8X4),
+                    lhsT_scale=xc_s[:, P * t : P * (t + 1)],
+                    rhs=z2_w[:, cols(h)].bitcast(FP8X4),
+                    rhs_scale=z2_s[:, cols(h)],
+                    start=True,
+                    stop=True,
+                )
+
+        a_part = [tile(f"a_part{t}", [P, W], F32) for t in range(PACK)]
+        for t in range(PACK):
+            nc.scalar.copy(out=res[t][:], in_=bank_ya[t][:])
+        for t in range(PACK - 1):
+            nc.vector.tensor_scalar(a_part[t][:], res[t][:].indirect(l_n6[:]), -0.5, 0.0, ALU.mult, ALU.add)
+        out_rows = out_0.rearrange("(p t) c -> p t c", t=PACK)
+        res_bf = [tile(f"res_bf{h}", [P, PACK, HALF], BF16) for h in range(2)]
+        b_part = [tile(f"b_part{t}", [P, W], F32) for t in range(PACK)]
+        for t in range(PACK):
+            nc.scalar.activation(out=b[t][:, cols(1)], in_=bank_db[t][:, cols(1)], func=ACT.Copy, scale=0.0625)
+            nc.scalar.activation(out=b_part[t][:], in_=b[t][:].indirect(l_n7[:]), func=ACT.Copy)
+        nc.scalar.activation(out=a_part[PACK - 1][:], in_=res[PACK - 1][:].indirect(l_n6[:]), func=ACT.Copy, scale=-0.5)
+        for t in range(PACK):
+            nc.vector.tensor_tensor(res[t][:].indirect(l_n6[:]), b_part[t][:], a_part[t][:], ALU.add)
+            nc.sync.dma_start(out_rows[:, t, :], res[t][:])
+            for h in range(2):
+                nc.scalar.copy(out=res_bf[h][:, t, :], in_=res[t][:, cols(h)])
+
+        o_w = tile("o_w", [P, S], U32)
+        o_s = tile("o_s", [P, S], U8)
+        o_bf = [tile(f"o_bf{h}", [P, PACK * HALF], BF16) for h in range(2)]
+        for h in range(2):
+            nc.vector.tensor_copy(woven(o_bf[h][:]), by_fours(res_bf[h][:]))
+        out_words = out_1[0].rearrange("p c r -> p (c r)").bitcast(I32)
+        for h in range(2):
+            nc.vector.quantize_mx(out=o_w[:, cols(h)].bitcast(FP8X4), scales=o_s[:, cols(h)], in_=o_bf[h][:])
+            nc.sync.dma_start(out_words[:, cols(h)], o_w[:, cols(h)].bitcast(I32))
+        for q in range(4):
+            eng = nc.scalar if q % 2 == 0 else nc.sync
+            eng.dma_start(out_2[0, 4 * q : 4 * q + 4, :].bitcast(I32), o_s[32 * q : 32 * q + 4, :].bitcast(I32))

@@ -19,6 +19,8 @@ T = 2048
 S = 512
 W = 256
 HALF = S // 2
+N2_SCALAR = (2, 2)
+X_EARLY = 512
 FLOPS = 4 * 2 * 512 * 512 * 512
 
 
@@ -56,12 +58,13 @@ def tile_picked_tfcdputbgmaxlerp_none_po_kernel(
             )
             return dealt
 
-        def deal_scales(name, raw):
+        def deal_scales(name, raw, parts):
             dealt = tile(name, [P, S], U8)
-            nc.vector.tensor_copy(
-                out=dealt[:].rearrange("p (t m) -> p t m", t=PACK),
-                in_=raw[:].rearrange("p (m t) -> p t m", t=PACK),
-            )
+            for ts in parts:
+                nc.vector.tensor_copy(
+                    out=dealt[:].rearrange("p (t m) -> p t m", t=PACK)[:, ts, :],
+                    in_=raw[:].rearrange("p (m t) -> p t m", t=PACK)[:, ts, :],
+                )
             return dealt
 
         def half(lst, h):
@@ -71,21 +74,23 @@ def tile_picked_tfcdputbgmaxlerp_none_po_kernel(
             return slice(HALF * h, HALF * (h + 1))
 
         def woven(ap):
-            return ap.rearrange("p (c i t) -> p c t i", i=4, t=PACK)
+            return ap.rearrange("p (c i t) -> p c t i", i=2, t=PACK)
 
         def by_fours(ap):
-            return ap.rearrange("p t (c i) -> p c t i", i=4)
+            return ap.rearrange("p t (c i) -> p c t i", i=2)
 
         xw = tile("xw", [P, T], U32)
         xs = tile("xs", [P, T], U8)
         wsr = [sb.tile([P, S], U8, name=f"wsr{i}", tag=f"shared{i}", align_bytes=64) for i in range(3)]
-        nc.gpsimd.memset(xs[:].bitcast(I32), 0)
+        nc.vector.memset(xs[:].bitcast(I32), 0)
         for i in range(3):
-            nc.vector.memset(wsr[i][:].bitcast(I32), 0)
+            nc.gpsimd.memset(wsr[i][:].bitcast(I32), 0)
+        x_src = x_words[0].rearrange("p c r -> p (c r)").bitcast(I32)
+        nc.sync.dma_start(xw[:, :X_EARLY].bitcast(I32), x_src[:, :X_EARLY])
         l_offs = load_list("l_offs", offs)
         l_two = load_list("l_two", two)
         load_scale_rows(xs, x_scales)
-        nc.sync.dma_start(xw[:].bitcast(I32), x_words[0].rearrange("p c r -> p (c r)").bitcast(I32))
+        nc.sync.dma_start(xw[:, X_EARLY:].bitcast(I32), x_src[:, X_EARLY:])
         w1r = load_weight_words("w1r", w1_words)
         w2r = load_weight_words("w2r", w2_words)
         w3r = load_weight_words("w3r", w3_words)
@@ -135,10 +140,10 @@ def tile_picked_tfcdputbgmaxlerp_none_po_kernel(
         w1w = deal_words("w1w", w1r)
         w2w = deal_words("w2w", w2r)
         w3w = deal_words("w3w", w3r)
-        w1s = deal_scales("w1s", wsr[0])
+        w1s = deal_scales("w1s", wsr[0], (slice(0, 1), slice(1, PACK)))
         xo_w, xo_s = pick("xo", l_offs, False, "xo_w")
         layer(bank_ya, w1w, w1s, xo_w, xo_s, whole)
-        w2s = deal_scales("w2s", wsr[1])
+        w2s = deal_scales("w2s", wsr[1], (slice(0, PACK),))
         xt_w, xt_s = pick("xt", l_two, False, "shared0")
         layer(bank_db, w2w, w2s, xt_w, xt_s, whole)
         xc_w, xc_s = pick("xc", l_cand, True, "xc_w")
@@ -156,8 +161,8 @@ def tile_picked_tfcdputbgmaxlerp_none_po_kernel(
 
         z_w = tile("z_w", [P, S], U32)
         z_s = tile("z_s", [P, S], U8)
-        w3s = deal_scales("w3s", wsr[2])
-        gn_b = gn_t[:].rearrange("p (c t i) -> p c t i", c=1, i=1).to_broadcast([P, HALF // 4, PACK, 4])
+        w3s = deal_scales("w3s", wsr[2], (slice(0, PACK),))
+        gn_b = gn_t[:].rearrange("p (c t i) -> p c t i", c=1, i=1).to_broadcast([P, HALF // 2, PACK, 2])
         dg = [tile(f"dg{t}", [P, S], F32) for t in range(PACK)]
         for h in range(2):
             gated = tile(f"gated{h}", [P, PACK, HALF], F32)
@@ -166,17 +171,17 @@ def tile_picked_tfcdputbgmaxlerp_none_po_kernel(
             for t in range(1, PACK):
                 nc.scalar.activation(out=gated[:, t, :], in_=y[t][:].indirect(half(l_n1, h)), func=ACT.Sigmoid)
                 nc.vector.tensor_tensor(gated[:, t, :], gated[:, t, :], y[t][:, cols(h)], ALU.mult)
-            for t in range(PACK - 1):
+            for t in range(N2_SCALAR[h]):
                 nc.scalar.activation(out=other[:, t, :], in_=y[t][:].indirect(half(l_n2, h)), func=ACT.Copy)
-            nc.vector.tensor_copy(other[:, PACK - 1, :], y[PACK - 1][:].indirect(half(l_n2, h)))
+            for t in range(N2_SCALAR[h], PACK):
+                nc.vector.tensor_copy(other[:, t, :], y[t][:].indirect(half(l_n2, h)))
             nc.vector.tensor_tensor(gated[:], gated[:], other[:], ALU.max)
             z_bf = tile(f"z_bf{h}", [P, PACK * HALF], BF16)
             nc.vector.tensor_tensor(woven(z_bf[:]), by_fours(gated[:]), gn_b, ALU.mult)
             nc.vector.quantize_mx(out=z_w[:, cols(h)].bitcast(FP8X4), scales=z_s[:, cols(h)], in_=z_bf[:])
             layer(bank_ya, w3w, w3s, z_w, z_s, cols(h))
 
-        nc.vector.tensor_scalar(dg[0][:], bank_db[0][:], gs_t[:, 0:1], None, ALU.mult)
-        for t in range(1, PACK):
+        for t in range(PACK):
             nc.scalar.activation(out=dg[t][:], in_=bank_db[t][:], func=ACT.Copy, scale=gs_t[:, t : t + 1])
         b = [tile(f"b{t}", [P, S], F32) for t in range(PACK)]
         res = [tile(f"res{t}", [P, S], F32) for t in range(PACK)]
@@ -198,7 +203,7 @@ def tile_picked_tfcdputbgmaxlerp_none_po_kernel(
                     nc.scalar.activation(out=b[t][:, cols(0)], in_=bank_db[t][:, cols(0)], func=ACT.Copy, scale=0.0625)
             for ts in (slice(0, PACK - 1), slice(PACK - 1, PACK)):
                 nc.vector.tensor_tensor(diff[:, ts, :], diff[:, ts, :], mix[:, ts, :], ALU.mult)
-            z2_bf = tile(f"z2_bf{h}", [P, PACK * HALF], BF16)
+            z2_bf = sb.tile([P, PACK * HALF], BF16, name=f"z2_bf{h}", tag=f"z2_bf{h}", align_bytes=64)
             nc.vector.tensor_tensor(woven(z2_bf[:]), by_fours(diff[:]), by_fours(pa[:]), ALU.add)
             nc.vector.quantize_mx(out=z2_w[:, cols(h)].bitcast(FP8X4), scales=z2_s[:, cols(h)], in_=z2_bf[:])
             for t in range(PACK):
@@ -212,33 +217,36 @@ def tile_picked_tfcdputbgmaxlerp_none_po_kernel(
                     stop=True,
                 )
 
-        a_part = [tile(f"a_part{t}", [P, W], F32) for t in range(PACK)]
+        a_part = sb.tile([P, PACK, W], F32, name="a_part", tag="z2_bf1", align_bytes=64)
         for t in range(PACK):
             nc.scalar.copy(out=res[t][:], in_=bank_ya[t][:])
-        for t in range(PACK - 1):
-            nc.vector.tensor_scalar(a_part[t][:], res[t][:].indirect(l_n6[:]), -0.5, 0.0, ALU.mult, ALU.add)
+        for t in range(PACK):
+            nc.vector.tensor_scalar(a_part[:, t, :], res[t][:].indirect(l_n6[:]), -0.5, 0.0, ALU.mult, ALU.add)
         out_rows = out_0.rearrange("(p t) c -> p t c", t=PACK)
-        res_bf = [tile(f"res_bf{h}", [P, PACK, HALF], BF16) for h in range(2)]
+        out_cols = (slice(0, 384), slice(384, S))
+        grouped = [tile(f"grouped{i}", [P, PACK, c.stop - c.start], F32) for i, c in enumerate(out_cols)]
         b_part = [tile(f"b_part{t}", [P, W], F32) for t in range(PACK)]
         for t in range(PACK):
             nc.scalar.activation(out=b[t][:, cols(1)], in_=bank_db[t][:, cols(1)], func=ACT.Copy, scale=0.0625)
             nc.scalar.activation(out=b_part[t][:], in_=b[t][:].indirect(l_n7[:]), func=ACT.Copy)
-        nc.scalar.activation(out=a_part[PACK - 1][:], in_=res[PACK - 1][:].indirect(l_n6[:]), func=ACT.Copy, scale=-0.5)
         for t in range(PACK):
-            nc.vector.tensor_tensor(res[t][:].indirect(l_n6[:]), b_part[t][:], a_part[t][:], ALU.add)
+            nc.vector.tensor_tensor(res[t][:].indirect(l_n6[:]), b_part[t][:], a_part[:, t, :], ALU.add)
             nc.sync.dma_start(out_rows[:, t, :], res[t][:])
-            for h in range(2):
-                nc.scalar.copy(out=res_bf[h][:, t, :], in_=res[t][:, cols(h)])
+            if t < PACK - 1:
+                nc.scalar.copy(out=grouped[0][:, t, :], in_=res[t][:, out_cols[0]])
+            else:
+                nc.vector.tensor_copy(grouped[0][:, t, :], res[t][:, out_cols[0]])
+            nc.scalar.copy(out=grouped[1][:, t, :], in_=res[t][:, out_cols[1]])
 
         o_w = tile("o_w", [P, S], U32)
         o_s = tile("o_s", [P, S], U8)
-        o_bf = [tile(f"o_bf{h}", [P, PACK * HALF], BF16) for h in range(2)]
-        for h in range(2):
-            nc.vector.tensor_copy(woven(o_bf[h][:]), by_fours(res_bf[h][:]))
+        o_bf = [tile(f"o_bf{i}", [P, PACK * (c.stop - c.start)], BF16) for i, c in enumerate(out_cols)]
+        nc.vector.tensor_copy(woven(o_bf[0][:]), by_fours(grouped[0][:]))
+        nc.scalar.copy(out=woven(o_bf[1][:]), in_=by_fours(grouped[1][:]))
         out_words = out_1[0].rearrange("p c r -> p (c r)").bitcast(I32)
-        for h in range(2):
-            nc.vector.quantize_mx(out=o_w[:, cols(h)].bitcast(FP8X4), scales=o_s[:, cols(h)], in_=o_bf[h][:])
-            nc.sync.dma_start(out_words[:, cols(h)], o_w[:, cols(h)].bitcast(I32))
+        for i, c in reversed(list(enumerate(out_cols))):
+            nc.vector.quantize_mx(out=o_w[:, c].bitcast(FP8X4), scales=o_s[:, c], in_=o_bf[i][:])
+            nc.sync.dma_start(out_words[:, c], o_w[:, c].bitcast(I32))
         for q in range(4):
             eng = nc.scalar if q % 2 == 0 else nc.sync
             eng.dma_start(out_2[0, 4 * q : 4 * q + 4, :].bitcast(I32), o_s[32 * q : 32 * q + 4, :].bitcast(I32))

@@ -19,7 +19,9 @@ T = 2048
 S = 512
 W = 256
 HALF = S // 2
-N2_SCALAR = (2, 2)
+D_PARTS = (slice(0, 256), slice(256, 512))
+A_VECTOR = 4
+N2_SCALAR = (2, 1)
 X_EARLY = 512
 FLOPS = 4 * 2 * 512 * 512 * 512
 
@@ -58,10 +60,10 @@ def tile_picked_tfcdputbgmaxlerp_none_po_kernel(
             )
             return dealt
 
-        def deal_scales(name, raw, parts):
+        def deal_scales(name, raw, parts, engine):
             dealt = tile(name, [P, S], U8)
             for ts in parts:
-                nc.vector.tensor_copy(
+                engine.tensor_copy(
                     out=dealt[:].rearrange("p (t m) -> p t m", t=PACK)[:, ts, :],
                     in_=raw[:].rearrange("p (m t) -> p t m", t=PACK)[:, ts, :],
                 )
@@ -69,6 +71,9 @@ def tile_picked_tfcdputbgmaxlerp_none_po_kernel(
 
         def half(lst, h):
             return lst[:, 16 * h : 16 * (h + 1)]
+
+        def entries(lst, c):
+            return lst[:, c.start // 16 : c.stop // 16]
 
         def cols(h):
             return slice(HALF * h, HALF * (h + 1))
@@ -140,17 +145,15 @@ def tile_picked_tfcdputbgmaxlerp_none_po_kernel(
         w1w = deal_words("w1w", w1r)
         w2w = deal_words("w2w", w2r)
         w3w = deal_words("w3w", w3r)
-        w1s = deal_scales("w1s", wsr[0], (slice(0, 1), slice(1, PACK)))
+        w1s = deal_scales("w1s", wsr[0], (slice(0, 1), slice(1, PACK)), nc.vector)
         xo_w, xo_s = pick("xo", l_offs, False, "xo_w")
         layer(bank_ya, w1w, w1s, xo_w, xo_s, whole)
-        w2s = deal_scales("w2s", wsr[1], (slice(0, PACK),))
+        w2s = deal_scales("w2s", wsr[1], (slice(0, PACK),), nc.gpsimd)
         xt_w, xt_s = pick("xt", l_two, False, "shared0")
         layer(bank_db, w2w, w2s, xt_w, xt_s, whole)
         xc_w, xc_s = pick("xc", l_cand, True, "xc_w")
 
         y = [tile(f"y{t}", [P, S], F32) for t in range(PACK)]
-        sig_y0 = tile("sig_y0", [P, S], F32)
-        nc.scalar.activation(out=sig_y0[:], in_=bank_ya[0][:], func=ACT.Sigmoid)
         for t in range(PACK):
             nc.scalar.copy(out=y[t][:], in_=bank_ya[t][:])
 
@@ -161,14 +164,13 @@ def tile_picked_tfcdputbgmaxlerp_none_po_kernel(
 
         z_w = tile("z_w", [P, S], U32)
         z_s = tile("z_s", [P, S], U8)
-        w3s = deal_scales("w3s", wsr[2], (slice(0, PACK),))
+        w3s = deal_scales("w3s", wsr[2], (slice(0, PACK),), nc.gpsimd)
         gn_b = gn_t[:].rearrange("p (c t i) -> p c t i", c=1, i=1).to_broadcast([P, HALF // 2, PACK, 2])
         dg = [tile(f"dg{t}", [P, S], F32) for t in range(PACK)]
         for h in range(2):
             gated = tile(f"gated{h}", [P, PACK, HALF], F32)
             other = tile(f"other{h}", [P, PACK, HALF], F32)
-            nc.vector.tensor_tensor(gated[:, 0, :], sig_y0[:].indirect(half(l_n1, h)), y[0][:, cols(h)], ALU.mult)
-            for t in range(1, PACK):
+            for t in range(PACK):
                 nc.scalar.activation(out=gated[:, t, :], in_=y[t][:].indirect(half(l_n1, h)), func=ACT.Sigmoid)
                 nc.vector.tensor_tensor(gated[:, t, :], gated[:, t, :], y[t][:, cols(h)], ALU.mult)
             for t in range(N2_SCALAR[h]):
@@ -181,56 +183,64 @@ def tile_picked_tfcdputbgmaxlerp_none_po_kernel(
             nc.vector.quantize_mx(out=z_w[:, cols(h)].bitcast(FP8X4), scales=z_s[:, cols(h)], in_=z_bf[:])
             layer(bank_ya, w3w, w3s, z_w, z_s, cols(h))
 
-        for t in range(PACK):
-            nc.scalar.activation(out=dg[t][:], in_=bank_db[t][:], func=ACT.Copy, scale=gs_t[:, t : t + 1])
         b = [tile(f"b{t}", [P, S], F32) for t in range(PACK)]
         res = [tile(f"res{t}", [P, S], F32) for t in range(PACK)]
         z2_w = tile("z2_w", [P, S], U32)
         z2_s = tile("z2_s", [P, S], U8)
-        for h in range(2):
-            pa = tile(f"pa{h}", [P, PACK, HALF], F32)
-            mix = tile(f"mix{h}", [P, PACK, HALF], F32)
-            diff = tile(f"diff{h}", [P, PACK, HALF], F32)
+
+        def empty_b(t, c):
+            nc.scalar.activation(out=b[t][:, c], in_=bank_db[t][:, c], func=ACT.Copy, scale=0.0625)
+
+        last = len(D_PARTS) - 1
+        for i, c in enumerate(D_PARTS):
+            n = c.stop - c.start
+            pa = tile(f"pa{i}", [P, PACK, n], F32)
+            mix = tile(f"mix{i}", [P, PACK, n], F32)
+            diff = tile(f"diff{i}", [P, PACK, n], F32)
             for t in range(PACK):
-                nc.scalar.activation(out=pa[:, t, :], in_=dg[t][:].indirect(half(l_n3, h)), func=ACT.Copy)
-                nc.vector.tensor_tensor(diff[:, t, :], dg[t][:].indirect(half(l_n5, h)), pa[:, t, :], ALU.subtract)
+                if i == 0:
+                    nc.scalar.activation(out=dg[t][:], in_=bank_db[t][:], func=ACT.Copy, scale=gs_t[:, t : t + 1])
+                nc.scalar.activation(out=pa[:, t, :], in_=dg[t][:].indirect(entries(l_n3, c)), func=ACT.Copy)
+                nc.vector.tensor_tensor(diff[:, t, :], dg[t][:].indirect(entries(l_n5, c)), pa[:, t, :], ALU.subtract)
             for t in range(PACK):
                 nc.scalar.activation(
-                    out=mix[:, t, :], in_=dg[t][:].indirect(half(l_n4, h)), func=ACT.Sigmoid, scale=gs_inv[:, t : t + 1]
+                    out=mix[:, t, :], in_=dg[t][:].indirect(entries(l_n4, c)), func=ACT.Sigmoid, scale=gs_inv[:, t : t + 1]
                 )
-            if h == 1:
-                for t in range(PACK):
-                    nc.scalar.activation(out=b[t][:, cols(0)], in_=bank_db[t][:, cols(0)], func=ACT.Copy, scale=0.0625)
             for ts in (slice(0, PACK - 1), slice(PACK - 1, PACK)):
                 nc.vector.tensor_tensor(diff[:, ts, :], diff[:, ts, :], mix[:, ts, :], ALU.mult)
-            z2_bf = sb.tile([P, PACK * HALF], BF16, name=f"z2_bf{h}", tag=f"z2_bf{h}", align_bytes=64)
+            z2_bf = sb.tile([P, PACK * n], BF16, name=f"z2_bf{i}", tag=f"z2_bf{i}", align_bytes=64)
             nc.vector.tensor_tensor(woven(z2_bf[:]), by_fours(diff[:]), by_fours(pa[:]), ALU.add)
-            nc.vector.quantize_mx(out=z2_w[:, cols(h)].bitcast(FP8X4), scales=z2_s[:, cols(h)], in_=z2_bf[:])
+            nc.vector.quantize_mx(out=z2_w[:, c].bitcast(FP8X4), scales=z2_s[:, c], in_=z2_bf[:])
+            if i == last:
+                for t in range(PACK):
+                    nc.scalar.copy(out=res[t][:], in_=bank_ya[t][:])
+                    empty_b(t, slice(0, c.start))
             for t in range(PACK):
                 nc.tensor.matmul_mx(
-                    out=bank_db[t][:, cols(h)],
+                    out=bank_db[t][:, c],
                     lhsT=xc_w[:, P * t : P * (t + 1)].bitcast(FP8X4),
                     lhsT_scale=xc_s[:, P * t : P * (t + 1)],
-                    rhs=z2_w[:, cols(h)].bitcast(FP8X4),
-                    rhs_scale=z2_s[:, cols(h)],
+                    rhs=z2_w[:, c].bitcast(FP8X4),
+                    rhs_scale=z2_s[:, c],
                     start=True,
                     stop=True,
                 )
 
-        a_part = sb.tile([P, PACK, W], F32, name="a_part", tag="z2_bf1", align_bytes=64)
-        for t in range(PACK):
-            nc.scalar.copy(out=res[t][:], in_=bank_ya[t][:])
-        for t in range(PACK):
-            nc.vector.tensor_scalar(a_part[:, t, :], res[t][:].indirect(l_n6[:]), -0.5, 0.0, ALU.mult, ALU.add)
+        a_vec = sb.tile([P, A_VECTOR, W], F32, name="a_vec", tag=f"z2_bf{last}", align_bytes=64)
+        a_part = [a_vec[:, t, :] if t < A_VECTOR else tile(f"a_part{t}", [P, W], F32)[:] for t in range(PACK)]
+        for t in range(A_VECTOR):
+            nc.vector.tensor_scalar(a_part[t], res[t][:].indirect(l_n6[:]), -0.5, 0.0, ALU.mult, ALU.add)
         out_rows = out_0.rearrange("(p t) c -> p t c", t=PACK)
         out_cols = (slice(0, 384), slice(384, S))
         grouped = [tile(f"grouped{i}", [P, PACK, c.stop - c.start], F32) for i, c in enumerate(out_cols)]
         b_part = [tile(f"b_part{t}", [P, W], F32) for t in range(PACK)]
         for t in range(PACK):
-            nc.scalar.activation(out=b[t][:, cols(1)], in_=bank_db[t][:, cols(1)], func=ACT.Copy, scale=0.0625)
+            empty_b(t, D_PARTS[last])
             nc.scalar.activation(out=b_part[t][:], in_=b[t][:].indirect(l_n7[:]), func=ACT.Copy)
+            if t >= A_VECTOR:
+                nc.scalar.activation(out=a_part[t], in_=res[t][:].indirect(l_n6[:]), func=ACT.Copy, scale=-0.5)
         for t in range(PACK):
-            nc.vector.tensor_tensor(res[t][:].indirect(l_n6[:]), b_part[t][:], a_part[:, t, :], ALU.add)
+            nc.vector.tensor_tensor(res[t][:].indirect(l_n6[:]), b_part[t][:], a_part[t], ALU.add)
             nc.sync.dma_start(out_rows[:, t, :], res[t][:])
             if t < PACK - 1:
                 nc.scalar.copy(out=grouped[0][:, t, :], in_=res[t][:, out_cols[0]])

@@ -19,8 +19,9 @@ T = 2048
 S = 512
 W = 256
 HALF = S // 2
+B_EARLY = 2
 D_PARTS = (slice(0, 256), slice(256, 512))
-A_VECTOR = 4
+A_VECTOR = 3
 N2_SCALAR = (2, 1)
 X_EARLY = 512
 FLOPS = 4 * 2 * 512 * 512 * 512
@@ -48,7 +49,7 @@ def tile_picked_tfcdputbgmaxlerp_none_po_kernel(
                 nc.sync.dma_start(dst[32 * q : 32 * q + 4, :].bitcast(I32), src[0, 4 * q : 4 * q + 4, :].bitcast(I32))
 
         def load_weight_words(name, src):
-            raw = tile(name, [P, 2 * S], U8)
+            raw = sb.tile([P, 2 * S], U8, name=name, tag=name, align_bytes=64)
             nc.sync.dma_start(raw[:].bitcast(I32), src[0].bitcast(I32))
             return raw
 
@@ -60,10 +61,10 @@ def tile_picked_tfcdputbgmaxlerp_none_po_kernel(
             )
             return dealt
 
-        def deal_scales(name, raw, parts, engine):
+        def deal_scales(name, raw, parts):
             dealt = tile(name, [P, S], U8)
             for ts in parts:
-                engine.tensor_copy(
+                nc.vector.tensor_copy(
                     out=dealt[:].rearrange("p (t m) -> p t m", t=PACK)[:, ts, :],
                     in_=raw[:].rearrange("p (m t) -> p t m", t=PACK)[:, ts, :],
                 )
@@ -79,10 +80,10 @@ def tile_picked_tfcdputbgmaxlerp_none_po_kernel(
             return slice(HALF * h, HALF * (h + 1))
 
         def woven(ap):
-            return ap.rearrange("p (c i t) -> p c t i", i=2, t=PACK)
+            return ap.rearrange("p (c i t) -> p c t i", i=4, t=PACK)
 
         def by_fours(ap):
-            return ap.rearrange("p t (c i) -> p c t i", i=2)
+            return ap.rearrange("p t (c i) -> p c t i", i=4)
 
         xw = tile("xw", [P, T], U32)
         xs = tile("xs", [P, T], U8)
@@ -96,10 +97,10 @@ def tile_picked_tfcdputbgmaxlerp_none_po_kernel(
         l_two = load_list("l_two", two)
         load_scale_rows(xs, x_scales)
         nc.sync.dma_start(xw[:, X_EARLY:].bitcast(I32), x_src[:, X_EARLY:])
+        load_scale_rows(wsr[0], w1_scales)
+        w3r = load_weight_words("w3r", w3_words)
         w1r = load_weight_words("w1r", w1_words)
         w2r = load_weight_words("w2r", w2_words)
-        w3r = load_weight_words("w3r", w3_words)
-        load_scale_rows(wsr[0], w1_scales)
         l_cand = load_list("l_cand", cand)
         l_n1 = load_list("l_n1", n1)
         l_n2 = load_list("l_n2", n2)
@@ -108,10 +109,10 @@ def tile_picked_tfcdputbgmaxlerp_none_po_kernel(
         gs_t = tile("gs_t", [P, PACK], F32)
         nc.sync.dma_start(gs_t[:], gs.rearrange("(p t) o -> p (t o)", t=PACK))
         nc.sync.dma_start(gn_t[:], gn.rearrange("(p t) o -> p (t o)", t=PACK))
-        load_scale_rows(wsr[2], w3_scales)
         l_n3 = load_list("l_n3", n3)
         l_n5 = load_list("l_n5", n5)
         l_n4 = load_list("l_n4", n4)
+        load_scale_rows(wsr[2], w3_scales)
         l_n6 = load_list("l_n6", n6)
         l_n7 = load_list("l_n7", n7)
 
@@ -145,12 +146,26 @@ def tile_picked_tfcdputbgmaxlerp_none_po_kernel(
         w1w = deal_words("w1w", w1r)
         w2w = deal_words("w2w", w2r)
         w3w = deal_words("w3w", w3r)
-        w1s = deal_scales("w1s", wsr[0], (slice(0, 1), slice(1, PACK)), nc.vector)
+        w1s = deal_scales("w1s", wsr[0], (slice(0, 1), slice(1, PACK)))
         xo_w, xo_s = pick("xo", l_offs, False, "xo_w")
         layer(bank_ya, w1w, w1s, xo_w, xo_s, whole)
-        w2s = deal_scales("w2s", wsr[1], (slice(0, PACK),), nc.gpsimd)
-        xt_w, xt_s = pick("xt", l_two, False, "shared0")
-        layer(bank_db, w2w, w2s, xt_w, xt_s, whole)
+        w2s = deal_scales("w2s", wsr[1], (slice(0, PACK),))
+        xt_s = [sb.tile([P, HALF], U8, name=f"xt_s{h}", tag=("xt_s0", "shared0")[h], align_bytes=64) for h in range(2)]
+        xt_w = sb.tile([P, S], U32, name="xt_w", tag="w1r", align_bytes=64)
+        for h in range(2):
+            nc.vector.tensor_copy(xt_s[h][:], xs[:].indirect(half(l_two, h)))
+        nc.vector.tensor_copy(xt_w[:], xw[:].indirect(l_two[:]))
+        for t in range(PACK):
+            for h in range(2):
+                nc.tensor.matmul_mx(
+                    out=bank_db[t][:, cols(h)],
+                    lhsT=w2w[:, 2 * P * t : 2 * P * (t + 1)].bitcast(FP4X4),
+                    lhsT_scale=w2s[:, P * t : P * (t + 1)],
+                    rhs=xt_w[:, cols(h)].bitcast(FP8X4),
+                    rhs_scale=xt_s[h][:],
+                    start=True,
+                    stop=True,
+                )
         xc_w, xc_s = pick("xc", l_cand, True, "xc_w")
 
         y = [tile(f"y{t}", [P, S], F32) for t in range(PACK)]
@@ -164,12 +179,12 @@ def tile_picked_tfcdputbgmaxlerp_none_po_kernel(
 
         z_w = tile("z_w", [P, S], U32)
         z_s = tile("z_s", [P, S], U8)
-        w3s = deal_scales("w3s", wsr[2], (slice(0, PACK),), nc.gpsimd)
-        gn_b = gn_t[:].rearrange("p (c t i) -> p c t i", c=1, i=1).to_broadcast([P, HALF // 2, PACK, 2])
+        w3s = deal_scales("w3s", wsr[2], (slice(0, PACK),))
+        gn_b = gn_t[:].rearrange("p (c t i) -> p c t i", c=1, i=1).to_broadcast([P, HALF // 4, PACK, 4])
         dg = [tile(f"dg{t}", [P, S], F32) for t in range(PACK)]
         for h in range(2):
             gated = tile(f"gated{h}", [P, PACK, HALF], F32)
-            other = tile(f"other{h}", [P, PACK, HALF], F32)
+            other = sb.tile([P, PACK, HALF], F32, name=f"other{h}", tag=f"other{h}", align_bytes=64)
             for t in range(PACK):
                 nc.scalar.activation(out=gated[:, t, :], in_=y[t][:].indirect(half(l_n1, h)), func=ACT.Sigmoid)
                 nc.vector.tensor_tensor(gated[:, t, :], gated[:, t, :], y[t][:, cols(h)], ALU.mult)
@@ -196,7 +211,7 @@ def tile_picked_tfcdputbgmaxlerp_none_po_kernel(
             n = c.stop - c.start
             pa = tile(f"pa{i}", [P, PACK, n], F32)
             mix = tile(f"mix{i}", [P, PACK, n], F32)
-            diff = tile(f"diff{i}", [P, PACK, n], F32)
+            diff = sb.tile([P, PACK, n], F32, name=f"diff{i}", tag="other1" if i == 0 else f"diff{i}", align_bytes=64)
             for t in range(PACK):
                 if i == 0:
                     nc.scalar.activation(out=dg[t][:], in_=bank_db[t][:], func=ACT.Copy, scale=gs_t[:, t : t + 1])
@@ -214,7 +229,8 @@ def tile_picked_tfcdputbgmaxlerp_none_po_kernel(
             if i == last:
                 for t in range(PACK):
                     nc.scalar.copy(out=res[t][:], in_=bank_ya[t][:])
-                    empty_b(t, slice(0, c.start))
+                    if t < B_EARLY:
+                        empty_b(t, slice(0, c.start))
             for t in range(PACK):
                 nc.tensor.matmul_mx(
                     out=bank_db[t][:, c],
@@ -226,8 +242,8 @@ def tile_picked_tfcdputbgmaxlerp_none_po_kernel(
                     stop=True,
                 )
 
-        a_vec = sb.tile([P, A_VECTOR, W], F32, name="a_vec", tag=f"z2_bf{last}", align_bytes=64)
-        a_part = [a_vec[:, t, :] if t < A_VECTOR else tile(f"a_part{t}", [P, W], F32)[:] for t in range(PACK)]
+        a_vec = sb.tile([P, PACK, W], F32, name="a_vec", tag=f"z2_bf{last}", align_bytes=64)
+        a_part = [a_vec[:, t, :] for t in range(PACK)]
         for t in range(A_VECTOR):
             nc.vector.tensor_scalar(a_part[t], res[t][:].indirect(l_n6[:]), -0.5, 0.0, ALU.mult, ALU.add)
         out_rows = out_0.rearrange("(p t) c -> p t c", t=PACK)
@@ -235,7 +251,7 @@ def tile_picked_tfcdputbgmaxlerp_none_po_kernel(
         grouped = [tile(f"grouped{i}", [P, PACK, c.stop - c.start], F32) for i, c in enumerate(out_cols)]
         b_part = [tile(f"b_part{t}", [P, W], F32) for t in range(PACK)]
         for t in range(PACK):
-            empty_b(t, D_PARTS[last])
+            empty_b(t, D_PARTS[last] if t < B_EARLY else whole)
             nc.scalar.activation(out=b_part[t][:], in_=b[t][:].indirect(l_n7[:]), func=ACT.Copy)
             if t >= A_VECTOR:
                 nc.scalar.activation(out=a_part[t], in_=res[t][:].indirect(l_n6[:]), func=ACT.Copy, scale=-0.5)

from contextlib import ExitStack

import concourse.mybir as mybir

F32 = mybir.dt.float32
BF16 = mybir.dt.bfloat16
I32 = mybir.dt.int32
U32 = mybir.dt.uint32
U16 = mybir.dt.uint16
U8 = mybir.dt.uint8
FP8X4 = mybir.dt.float8_e4m3fn_x4
FP4X4 = mybir.dt.float4_e2m1fn_x4
ALU = mybir.AluOpType
ACT = mybir.ActivationFunctionType

P = 128
PACK = 4
T = 2048
S = 512
W = 256
HALF = S // 2
B_EARLY = 2
D_PARTS = (slice(0, 256), slice(256, 512))
A_VECTOR = 3
N2_SCALAR = (2, 1)
X_EARLY = 512
FLOPS = 4 * 2 * 512 * 512 * 512


def tile_picked_tfcdputbgmaxlerp_none_po_kernel(
    tc, x_words, x_scales, w1_words, w1_scales, w2_words, w2_scales, gn, w3_words, w3_scales, gs,
    offs, two, n1, n2, n3, n4, n5, cand, n6, n7, out_0, out_1, out_2,
):
    nc = tc.nc
    with ExitStack() as ctx:
        sb = ctx.enter_context(tc.tile_pool(name="sb", bufs=1))
        ps = ctx.enter_context(tc.psum_pool(name="ps", bufs=1))

        def tile(name, shape, dtype):
            return sb.tile(shape, dtype, name=name, align_bytes=64)

        def load_list(name, src):
            t = sb.tile(list(src.shape), U16, name=name)
            nc.sync.dma_start(t[:], src)
            return t

        def load_scale_rows(dst, src):
            for q in range(4):
                nc.sync.dma_start(dst[32 * q : 32 * q + 4, :].bitcast(I32), src[0, 4 * q : 4 * q + 4, :].bitcast(I32))

        def load_weight_words(name, src):
            raw = sb.tile([P, 2 * S], U8, name=name, tag=name, align_bytes=64)
            nc.sync.dma_start(raw[:].bitcast(I32), src[0].bitcast(I32))
            return raw

        def deal_words(name, raw):
            dealt = tile(name, [P, 2 * S], U8)
            nc.scalar.copy(
                out=dealt[:].bitcast(U16).rearrange("p (t m) -> p t m", t=PACK),
                in_=raw[:].bitcast(U16).rearrange("p (m t) -> p t m", t=PACK),
            )
            return dealt

        def deal_scales(name, raw, parts):
            dealt = tile(name, [P, S], U8)
            for ts in parts:
                nc.vector.tensor_copy(
                    out=dealt[:].rearrange("p (t m) -> p t m", t=PACK)[:, ts, :],
                    in_=raw[:].rearrange("p (m t) -> p t m", t=PACK)[:, ts, :],
                )
            return dealt

        def half(lst, h):
            return lst[:, 16 * h : 16 * (h + 1)]

        def entries(lst, c):
            return lst[:, c.start // 16 : c.stop // 16]

        def cols(h):
            return slice(HALF * h, HALF * (h + 1))

        def woven(ap):
            return ap.rearrange("p (c i t) -> p c t i", i=4, t=PACK)

        def by_fours(ap):
            return ap.rearrange("p t (c i) -> p c t i", i=4)

        xw = tile("xw", [P, T], U32)
        xs = tile("xs", [P, T], U8)
        wsr = [sb.tile([P, S], U8, name=f"wsr{i}", tag=f"shared{i}", align_bytes=64) for i in range(3)]
        nc.vector.memset(xs[:].bitcast(I32), 0)
        for i in range(3):
            nc.gpsimd.memset(wsr[i][:].bitcast(I32), 0)
        x_src = x_words[0].rearrange("p c r -> p (c r)").bitcast(I32)
        nc.sync.dma_start(xw[:, :X_EARLY].bitcast(I32), x_src[:, :X_EARLY])
        l_offs = load_list("l_offs", offs)
        l_two = load_list("l_two", two)
        load_scale_rows(xs, x_scales)
        nc.sync.dma_start(xw[:, X_EARLY:].bitcast(I32), x_src[:, X_EARLY:])
        load_scale_rows(wsr[0], w1_scales)
        w3r = load_weight_words("w3r", w3_words)
        w1r = load_weight_words("w1r", w1_words)
        w2r = load_weight_words("w2r", w2_words)
        l_cand = load_list("l_cand", cand)
        l_n1 = load_list("l_n1", n1)
        l_n2 = load_list("l_n2", n2)
        load_scale_rows(wsr[1], w2_scales)
        gn_t = tile("gn_t", [P, PACK], F32)
        gs_t = tile("gs_t", [P, PACK], F32)
        nc.sync.dma_start(gs_t[:], gs.rearrange("(p t) o -> p (t o)", t=PACK))
        nc.sync.dma_start(gn_t[:], gn.rearrange("(p t) o -> p (t o)", t=PACK))
        l_n3 = load_list("l_n3", n3)
        l_n5 = load_list("l_n5", n5)
        l_n4 = load_list("l_n4", n4)
        load_scale_rows(wsr[2], w3_scales)
        l_n6 = load_list("l_n6", n6)
        l_n7 = load_list("l_n7", n7)

        bank_ya = [ps.tile([P, S], F32, name=f"bank_ya{t}") for t in range(PACK)]
        bank_db = [ps.tile([P, S], F32, name=f"bank_db{t}") for t in range(PACK)]

        def pick(name, lst, dealt, tag):
            words = sb.tile([P, S], U32, name=name + "_w", tag=tag, align_bytes=64)
            scales = tile(name + "_s", [P, S], U8)
            ow, os_ = words[:], scales[:]
            if dealt:
                ow = ow.rearrange("p (t m) -> p m t", t=PACK)
                os_ = os_.rearrange("p (t m) -> p m t", t=PACK)
            nc.vector.tensor_copy(os_, xs[:].indirect(lst[:]))
            nc.vector.tensor_copy(ow, xw[:].indirect(lst[:]))
            return words, scales

        def layer(banks, w_words, w_scales, words, scales, c):
            for t in range(PACK):
                nc.tensor.matmul_mx(
                    out=banks[t][:, c],
                    lhsT=w_words[:, 2 * P * t : 2 * P * (t + 1)].bitcast(FP4X4),
                    lhsT_scale=w_scales[:, P * t : P * (t + 1)],
                    rhs=words[:, c].bitcast(FP8X4),
                    rhs_scale=scales[:, c],
                    start=True,
                    stop=True,
                )

        whole = slice(0, S)
        w1w = deal_words("w1w", w1r)
        w2w = deal_words("w2w", w2r)
        w3w = deal_words("w3w", w3r)
        w1s = deal_scales("w1s", wsr[0], (slice(0, 1), slice(1, PACK)))
        xo_w, xo_s = pick("xo", l_offs, False, "xo_w")
        layer(bank_ya, w1w, w1s, xo_w, xo_s, whole)
        w2s = deal_scales("w2s", wsr[1], (slice(0, PACK),))
        xt_s = [sb.tile([P, HALF], U8, name=f"xt_s{h}", tag=("xt_s0", "shared0")[h], align_bytes=64) for h in range(2)]
        xt_w = sb.tile([P, S], U32, name="xt_w", tag="w1r", align_bytes=64)
        for h in range(2):
            nc.vector.tensor_copy(xt_s[h][:], xs[:].indirect(half(l_two, h)))
        nc.vector.tensor_copy(xt_w[:], xw[:].indirect(l_two[:]))
        for t in range(PACK):
            for h in range(2):
                nc.tensor.matmul_mx(
                    out=bank_db[t][:, cols(h)],
                    lhsT=w2w[:, 2 * P * t : 2 * P * (t + 1)].bitcast(FP4X4),
                    lhsT_scale=w2s[:, P * t : P * (t + 1)],
                    rhs=xt_w[:, cols(h)].bitcast(FP8X4),
                    rhs_scale=xt_s[h][:],
                    start=True,
                    stop=True,
                )
        xc_w, xc_s = pick("xc", l_cand, True, "xc_w")

        y = [tile(f"y{t}", [P, S], F32) for t in range(PACK)]
        for t in range(PACK):
            nc.scalar.copy(out=y[t][:], in_=bank_ya[t][:])

        gs_inv = tile("gs_inv", [P, PACK], F32)
        gs_safe = tile("gs_safe", [P, PACK], F32)
        nc.vector.scalar_tensor_tensor(gs_safe[:], gs_t[:], 0.0, gs_t[:], ALU.is_equal, ALU.add)
        nc.vector.reciprocal(gs_inv[:], gs_safe[:])

        z_w = tile("z_w", [P, S], U32)
        z_s = tile("z_s", [P, S], U8)
        w3s = deal_scales("w3s", wsr[2], (slice(0, PACK),))
        gn_b = gn_t[:].rearrange("p (c t i) -> p c t i", c=1, i=1).to_broadcast([P, HALF // 4, PACK, 4])
        dg = [tile(f"dg{t}", [P, S], F32) for t in range(PACK)]
        for h in range(2):
            gated = tile(f"gated{h}", [P, PACK, HALF], F32)
            other = sb.tile([P, PACK, HALF], F32, name=f"other{h}", tag=f"other{h}", align_bytes=64)
            for t in range(PACK):
                nc.scalar.activation(out=gated[:, t, :], in_=y[t][:].indirect(half(l_n1, h)), func=ACT.Sigmoid)
                nc.vector.tensor_tensor(gated[:, t, :], gated[:, t, :], y[t][:, cols(h)], ALU.mult)
            for t in range(N2_SCALAR[h]):
                nc.scalar.activation(out=other[:, t, :], in_=y[t][:].indirect(half(l_n2, h)), func=ACT.Copy)
            for t in range(N2_SCALAR[h], PACK):
                nc.vector.tensor_copy(other[:, t, :], y[t][:].indirect(half(l_n2, h)))
            nc.vector.tensor_tensor(gated[:], gated[:], other[:], ALU.max)
            z_bf = tile(f"z_bf{h}", [P, PACK * HALF], BF16)
            nc.vector.tensor_tensor(woven(z_bf[:]), by_fours(gated[:]), gn_b, ALU.mult)
            nc.vector.quantize_mx(out=z_w[:, cols(h)].bitcast(FP8X4), scales=z_s[:, cols(h)], in_=z_bf[:])
            layer(bank_ya, w3w, w3s, z_w, z_s, cols(h))

        b = [tile(f"b{t}", [P, S], F32) for t in range(PACK)]
        res = [tile(f"res{t}", [P, S], F32) for t in range(PACK)]
        z2_w = tile("z2_w", [P, S], U32)
        z2_s = tile("z2_s", [P, S], U8)

        def empty_b(t, c):
            nc.scalar.activation(out=b[t][:, c], in_=bank_db[t][:, c], func=ACT.Copy, scale=0.0625)

        last = len(D_PARTS) - 1
        for i, c in enumerate(D_PARTS):
            n = c.stop - c.start
            pa = tile(f"pa{i}", [P, PACK, n], F32)
            mix = tile(f"mix{i}", [P, PACK, n], F32)
            diff = sb.tile([P, PACK, n], F32, name=f"diff{i}", tag="other1" if i == 0 else f"diff{i}", align_bytes=64)
            for t in range(PACK):
                if i == 0:
                    nc.scalar.activation(out=dg[t][:], in_=bank_db[t][:], func=ACT.Copy, scale=gs_t[:, t : t + 1])
                nc.scalar.activation(out=pa[:, t, :], in_=dg[t][:].indirect(entries(l_n3, c)), func=ACT.Copy)
                nc.vector.tensor_tensor(diff[:, t, :], dg[t][:].indirect(entries(l_n5, c)), pa[:, t, :], ALU.subtract)
            for t in range(PACK):
                nc.scalar.activation(
                    out=mix[:, t, :], in_=dg[t][:].indirect(entries(l_n4, c)), func=ACT.Sigmoid, scale=gs_inv[:, t : t + 1]
                )
            for ts in (slice(0, PACK - 1), slice(PACK - 1, PACK)):
                nc.vector.tensor_tensor(diff[:, ts, :], diff[:, ts, :], mix[:, ts, :], ALU.mult)
            z2_bf = sb.tile([P, PACK * n], BF16, name=f"z2_bf{i}", tag=f"z2_bf{i}", align_bytes=64)
            nc.vector.tensor_tensor(woven(z2_bf[:]), by_fours(diff[:]), by_fours(pa[:]), ALU.add)
            nc.vector.quantize_mx(out=z2_w[:, c].bitcast(FP8X4), scales=z2_s[:, c], in_=z2_bf[:])
            if i == last:
                for t in range(PACK):
                    nc.scalar.copy(out=res[t][:], in_=bank_ya[t][:])
                    if t < B_EARLY:
                        empty_b(t, slice(0, c.start))
            for t in range(PACK):
                nc.tensor.matmul_mx(
                    out=bank_db[t][:, c],
                    lhsT=xc_w[:, P * t : P * (t + 1)].bitcast(FP8X4),
                    lhsT_scale=xc_s[:, P * t : P * (t + 1)],
                    rhs=z2_w[:, c].bitcast(FP8X4),
                    rhs_scale=z2_s[:, c],
                    start=True,
                    stop=True,
                )

        a_vec = sb.tile([P, PACK, W], F32, name="a_vec", tag=f"z2_bf{last}", align_bytes=64)
        a_part = [a_vec[:, t, :] for t in range(PACK)]
        for t in range(A_VECTOR):
            nc.vector.tensor_scalar(a_part[t], res[t][:].indirect(l_n6[:]), -0.5, 0.0, ALU.mult, ALU.add)
        out_rows = out_0.rearrange("(p t) c -> p t c", t=PACK)
        out_cols = (slice(0, 384), slice(384, S))
        grouped = [tile(f"grouped{i}", [P, PACK, c.stop - c.start], F32) for i, c in enumerate(out_cols)]
        b_part = [tile(f"b_part{t}", [P, W], F32) for t in range(PACK)]
        for t in range(PACK):
            empty_b(t, D_PARTS[last] if t < B_EARLY else whole)
            nc.scalar.activation(out=b_part[t][:], in_=b[t][:].indirect(l_n7[:]), func=ACT.Copy)
            if t >= A_VECTOR:
                nc.scalar.activation(out=a_part[t], in_=res[t][:].indirect(l_n6[:]), func=ACT.Copy, scale=-0.5)
        for t in range(PACK):
            nc.vector.tensor_tensor(res[t][:].indirect(l_n6[:]), b_part[t][:], a_part[t], ALU.add)
            nc.sync.dma_start(out_rows[:, t, :], res[t][:])
            if t < PACK - 1:
                nc.scalar.copy(out=grouped[0][:, t, :], in_=res[t][:, out_cols[0]])
            else:
                nc.vector.tensor_copy(grouped[0][:, t, :], res[t][:, out_cols[0]])
            nc.scalar.copy(out=grouped[1][:, t, :], in_=res[t][:, out_cols[1]])

        o_w = tile("o_w", [P, S], U32)
        o_s = tile("o_s", [P, S], U8)
        o_bf = [tile(f"o_bf{i}", [P, PACK * (c.stop - c.start)], BF16) for i, c in enumerate(out_cols)]
        nc.vector.tensor_copy(woven(o_bf[0][:]), by_fours(grouped[0][:]))
        nc.scalar.copy(out=woven(o_bf[1][:]), in_=by_fours(grouped[1][:]))
        out_words = out_1[0].rearrange("p c r -> p (c r)").bitcast(I32)
        for i, c in reversed(list(enumerate(out_cols))):
            nc.vector.quantize_mx(out=o_w[:, c].bitcast(FP8X4), scales=o_s[:, c], in_=o_bf[i][:])
            nc.sync.dma_start(out_words[:, c], o_w[:, c].bitcast(I32))
        for q in range(4):
            eng = nc.scalar if q % 2 == 0 else nc.sync
            eng.dma_start(out_2[0, 4 * q : 4 * q + 4, :].bitcast(I32), o_s[32 * q : 32 * q + 4, :].bitcast(I32))
